import numpy as np
import ml_dtypes


def mxq(x, axis, fmt="e4m3"):
    dtype, down = {"e4m3": (ml_dtypes.float8_e4m3fn, 7), "e5m2": (ml_dtypes.float8_e5m2, 14)}[fmt]
    v = np.moveaxis(np.asarray(x, np.float32).astype(ml_dtypes.bfloat16).astype(np.float64), axis, -1)
    blocks = v.reshape(v.shape[:-1] + (-1, 32))
    amax = np.abs(blocks).max(-1, keepdims=True)
    byte = np.maximum(np.where(amax > 0, np.frexp(amax)[1] - 1 + 127, 0) - down, 1)
    scale = np.exp2(byte - 127.0)
    codes = (blocks / scale).astype(np.float32).astype(dtype).astype(np.float64)
    return np.moveaxis((codes * scale).reshape(v.shape), -1, axis)


WIDE = False


def mx_kscale(k):
    if not WIDE:
        return np.ones(k)
    levels = np.array([10, -10, 5, -5, 0])
    if k % 512:
        return np.exp2(np.random.permutation(np.resize(levels, k // 32))).repeat(32)
    a = np.empty((k // 512, 16))
    for p in range(k // 512):
        a[p, :8] = np.random.permutation(np.resize(levels, 8))
        for g in range(8):
            far = levels[np.abs(levels - a[p, g]) >= 10]
            a[p, g + 8] = far[np.random.randint(len(far))]
    return np.exp2(a.ravel()).repeat(32)


def f64(x):
    return np.asarray(x).astype(np.float64)


def striped(idx):
    return np.tile(idx.reshape(-1, 16).T, (8, 1)).astype(np.uint16)


def unstriped(offs):
    return offs[:16].T.reshape(-1).astype(np.int64)


E2M1 = np.array([0.0, 0.5, 1.0, 1.5, 2.0, 3.0, 4.0, 6.0, -0.0, -0.5, -1.0, -1.5, -2.0, -3.0, -4.0, -6.0])


def pack_weight(w, fmt):
    k, n = w.shape
    w = f64(np.asarray(w, np.float32).astype(ml_dtypes.bfloat16)).reshape(k // 32, 32, n)
    amax = np.abs(w).max(1)
    if fmt == "e4m3":
        byte = np.frexp(amax)[1] - 1 + 127 - 7
    else:
        mant, ex = np.frexp(amax / 6.0)
        byte = np.where(mant > 0.5, ex, ex - 1) + 127
    byte = np.clip(np.where(amax > 0, byte, 1), 1, 254)
    scaled = (w * np.exp2(127.0 - byte)[:, None, :]).reshape(k, n).astype(np.float32)
    by_word = np.ascontiguousarray(scaled.reshape(k // 512, 128, 4, n).transpose(0, 1, 3, 2))
    if fmt == "e4m3":
        words = by_word.astype(ml_dtypes.float8_e4m3fn).view(np.uint8)
    else:
        c = by_word.astype(ml_dtypes.float4_e2m1fn).view(np.uint8) & 0xF
        words = (c[..., 0::2] | (c[..., 1::2] << 4)).reshape(k // 512, 128, 2 * n)
    return np.ascontiguousarray(words), np.ascontiguousarray(byte.astype(np.uint8).reshape(k // 512, 16, n))


def unpack_weight(words, scales, fmt):
    g, _, n = scales.shape
    words = np.ascontiguousarray(words).reshape(g, 128, n, -1)
    if fmt == "e4m3":
        vals = words.view(ml_dtypes.float8_e4m3fn).astype(np.float64)
    else:
        nib = np.empty((g, 128, n, 4), np.uint8)
        nib[..., 0::2] = words & 0xF
        nib[..., 1::2] = words >> 4
        vals = E2M1[nib]
    vals = vals * np.repeat(np.exp2(scales.astype(np.float64) - 127.0), 8, axis=1)[..., None]
    return vals.transpose(0, 1, 3, 2).reshape(g * 512, n)


def planes(y):
    n, m = y.shape
    v = y.astype(np.float32).astype(ml_dtypes.bfloat16).astype(np.float64).reshape(n // 32, 32, m)
    top = np.abs(v).max(1)
    byte = np.clip(np.where(top > 0, np.frexp(top)[1] - 1 + 127 - 7, 1), 1, 254)
    codes = (v * np.exp2(127.0 - byte)[:, None, :]).reshape(n, m).astype(np.float32).astype(ml_dtypes.float8_e4m3fn).view(np.uint8)
    words = codes.reshape(n // 512, 128, 4, m).transpose(0, 1, 3, 2)
    return np.ascontiguousarray(words), np.ascontiguousarray(byte.astype(np.uint8).reshape(n // 512, 16, m))


def gelu(v):
    return 0.5 * v * (1.0 + np.tanh(np.sqrt(2.0 / np.pi) * (v + 0.044715 * v**3)))


K, T, E1, C1, E2, C2, H = 1536, 768, 6, 128, 3, 256, 512
N = 512


def deal(E, C):
    slot_token = np.random.permutation(T)
    return slot_token, None, np.random.uniform(0.2, 1.0, T)


def by_expert(wq, xq, E, C):
    return np.concatenate([wq[e].T @ xq[:, e * C:(e + 1) * C] for e in range(E)], axis=1)


def setup_inputs():
    n = np.random.standard_normal
    s = mx_kscale(K)
    u = mx_kscale(H)
    slots1, pos1, g1 = deal(E1, C1)
    slots2, pos2, g2 = deal(E2, C2)
    x = pack_weight(n((K, T)) * s[:, None], "e4m3")
    w1 = [pack_weight(m, "e2m1") for m in n((E1, K, H)) / np.sqrt(K) / s[None, :, None] * u]
    return {
        "x_words": x[0],
        "x_scales": x[1],
        "w1_words": np.stack([m[0] for m in w1]),
        "w1_scales": np.stack([m[1] for m in w1]),
        "w2": (n((E2, H, N)) / np.sqrt(H) / u[None, :, None]).astype(np.float32),
        "gate1": (np.tile(g1, (128, 1))).astype(np.float32),
        "gate2": (np.tile(g2, (128, 1))).astype(np.float32),
        "offs": striped(slots1),
        "offs2": striped(slots2),
    }


def reference(x_words, x_scales, w1_words, w1_scales, w2, gate1, gate2, offs, offs2):
    w1 = np.stack([unpack_weight(w1_words[e], w1_scales[e], "e2m1") for e in range(E1)])
    w2q = mxq(f64(w2), 1, "e4m3")
    idx, idx2 = unstriped(offs), unstriped(offs2)
    xq = unpack_weight(x_words, x_scales, "e4m3")[:, idx]
    h = gelu(by_expert(w1, xq, E1, C1))
    c = np.zeros((H, T))
    c[:, idx] = f64(gate1[:1]) * h
    y = by_expert(w2q, mxq(c[:, idx2], 0, "e4m3"), E2, C2)
    out = np.zeros((N, T))
    out[:, idx2] = f64(gate2[:1]) * y
    out_0 = out
    return (out_0,) + planes(out_0)

@@ -1,0 +1,244 @@
+from contextlib import ExitStack
+
+import concourse.mybir as mybir
+from concourse.masks import make_identity
+
+K, T, H, N = 1536, 768, 512, 512
+E1, C1 = 6, 128
+E2, C2 = 3, 256
+FLOPS = 2 * T * K * H + 2 * T * H * N
+
+F32 = mybir.dt.float32
+BF16 = mybir.dt.bfloat16
+I32 = mybir.dt.int32
+U32 = mybir.dt.uint32
+U16 = mybir.dt.uint16
+U8 = mybir.dt.uint8
+FP8X4 = mybir.dt.float8_e4m3fn_x4
+FP4X4 = mybir.dt.float4_e2m1fn_x4
+ACT = mybir.ActivationFunctionType
+MULT = mybir.AluOpType.mult
+
+P = 128
+PACK = 4
+PASSES = K // (P * PACK)
+CHUNK = 256
+CHUNKS = T // CHUNK
+COLS = CHUNK // 16
+WIDE = 1024
+
+
+def tile_moe_ser_gelu_kernel(
+    tc, x_words, x_scales, w1_words, w1_scales, w2, gate1, gate2, offs, offs2, out_0, out_1, out_2
+):
+    nc = tc.nc
+    with ExitStack() as ctx:
+        lists = ctx.enter_context(tc.tile_pool(name="lists", bufs=1))
+        keep = ctx.enter_context(tc.tile_pool(name="keep", bufs=1))
+        ring = ctx.enter_context(tc.tile_pool(name="ring", bufs=3))
+        psum = ctx.enter_context(tc.psum_pool(name="psum", bufs=1))
+
+        list1 = lists.tile([P, T // 16], U16, name="list1")
+        list2 = lists.tile([P, T // 16], U16, name="list2")
+
+        xs = keep.tile([P, PASSES * T], U8, name="xs", align_bytes=64)
+        nc.gpsimd.memset(xs[:].bitcast(I32), 0)
+        w1s = keep.tile([P, E1 * PASSES * H], U8, name="w1s", align_bytes=64)
+        nc.vector.memset(w1s[:].bitcast(I32), 0)
+        g1rows = keep.tile([P, P], F32, name="g1rows", tag="a", align_bytes=64)
+        nc.gpsimd.memset(g1rows[:], 0.0)
+        nc.gpsimd.dma_start(g1rows[0:E1, :], gate1[0].rearrange("(e u) -> e u", e=E1))
+        ident = keep.tile([P, P], F32, name="ident")
+        make_identity(nc, ident[:])
+        warm = keep.tile([P, 1], F32, name="warm")
+        nc.scalar.activation(warm[:], ident[:, 0:1], ACT.Gelu_apprx_tanh)
+
+        nc.sync.dma_start(list1[:], offs)
+        nc.sync.dma_start(list2[:], offs2)
+        x_rows = x_words.rearrange("s p t d -> p s (t d)").bitcast(I32)
+        xw0 = keep.tile([P, T], I32, name="xw0", tag="b", align_bytes=64)
+        nc.sync.dma_start(xw0[:], x_rows[:, 0, :])
+        xw = keep.tile([P, (PASSES - 1) * T], I32, name="xw", tag="c", align_bytes=64)
+        nc.sync.dma_start(xw[:].rearrange("p (s t) -> p s t", s=PASSES - 1), x_rows[:, 1:PASSES, :])
+        xs_rows = x_scales.rearrange("s (q r) t -> r q s t", r=4)
+        for r in range(4):
+            nc.sync.dma_start(
+                xs[r:P:32, :].bitcast(I32).rearrange("q (s t) -> q s t", s=PASSES), xs_rows[r].bitcast(I32)
+            )
+        w1s_rows = w1_scales.rearrange("e s (q r) n -> r q (e s) n", r=4)
+
+        def load_w1_scales(e0, e1):
+            g0, g1 = e0 * PASSES, e1 * PASSES
+            for r in range(4):
+                nc.sync.dma_start(
+                    w1s[r:P:32, g0 * H : g1 * H].bitcast(I32).rearrange("q (g n) -> q g n", g=g1 - g0),
+                    w1s_rows[r][:, g0:g1, :].bitcast(I32),
+                )
+
+
+        w1w = []
+        w2raw = []
+
+        def load_w1(k):
+            w1w.append(keep.tile([P, 2 * PASSES * 2 * H], U8, name="w1w%d" % k, tag="eba"[k], align_bytes=64))
+            nc.sync.dma_start(
+                w1w[k][:].bitcast(I32).rearrange("p (g n) -> p g n", g=2 * PASSES),
+                w1_words[2 * k : 2 * k + 2].rearrange("e s p n -> p (e s) n").bitcast(I32),
+            )
+
+        def load_w2(f):
+            w2raw.append(keep.tile([P, PACK, N], F32, name="w2raw%d" % f, tag="ceb"[f], align_bytes=64))
+            nc.sync.dma_start(w2raw[f][:], w2[f].rearrange("(p j) n -> p j n", j=PACK))
+
+        load_w1(0)
+        load_w1_scales(0, E1)
+
+        gt = psum.tile([P, P], F32, name="gt", tag="tr", bufs=2)
+        nc.tensor.transpose(gt[:], g1rows[:], ident[:])
+        g1 = keep.tile([P, 8], F32, name="g1")
+        nc.scalar.copy(g1[:, 0:E1], gt[:, 0:E1])
+
+        xg0 = keep.tile([P, T], U32, name="xg0", tag="d", align_bytes=64)
+        for a in range(0, T, T // 2):
+            nc.vector.tensor_copy(
+                xg0[:, a : a + T // 2], xw0[:].bitcast(U32).indirect(list1[:, a // 16 : (a + T // 2) // 16])
+            )
+        load_w1(1)
+        load_w1(2)
+        xg12 = keep.tile([P, (PASSES - 1) * T], U32, name="xg12", align_bytes=64)
+        for s in range(PASSES - 1):
+            for a in range(0, T, T // 2):
+                nc.vector.tensor_copy(
+                    xg12[:, s * T + a : s * T + a + T // 2],
+                    xw[:, s * T : (s + 1) * T].bitcast(U32).indirect(list1[:, a // 16 : (a + T // 2) // 16]),
+                )
+        load_w2(0)
+        xg = [xg0[:], xg12[:, 0:T], xg12[:, T : 2 * T]]
+        sg = [keep.tile([P, T], U8, name="sg%d" % s, align_bytes=64) for s in range(PASSES)]
+        for a in range(0, T, CHUNK):
+            for s in range(PASSES):
+                nc.vector.tensor_copy(
+                    sg[s][:, a : a + CHUNK], xs[:, s * T : (s + 1) * T].indirect(list1[:, a // 16 : (a + CHUNK) // 16])
+                )
+
+        w2q = [keep.tile([P, N], U32, name="w2q%d" % f, align_bytes=64) for f in range(E2)]
+        w2s = [keep.tile([P, N], U8, name="w2s%d" % f, align_bytes=64) for f in range(E2)]
+
+        cwin = [keep.tile([P, T], F32, name="cwin%d" % u) for u in range(2)]
+        for e in range(E1):
+            k, ee = divmod(e, 2)
+            slots = slice(e * C1, (e + 1) * C1)
+            acc = psum.tile([P, H], F32, name="acc", tag="acc", bufs=3)
+            for s in range(PASSES):
+                g = ee * PASSES + s
+                nc.tensor.matmul_mx(
+                    out=acc[:],
+                    lhsT=xg[s][:, slots].bitcast(FP8X4),
+                    lhsT_scale=sg[s][:, slots],
+                    rhs=w1w[k][:, g * 2 * H : (g + 1) * 2 * H].bitcast(FP4X4),
+                    rhs_scale=w1s[:, (e * PASSES + s) * H : (e * PASSES + s + 1) * H],
+                    start=(s == 0),
+                    stop=(s == PASSES - 1),
+                )
+            if e in (1, 3):
+                load_w2((e + 1) // 2)
+            hs = ring.tile([P, H], F32, name="hs")
+            nc.scalar.activation(
+                hs[:].rearrange("s (u p d) -> s u p d", u=2, d=2),
+                acc[:].rearrange("s (p u d) -> s u p d", u=2, d=2),
+                ACT.Gelu_apprx_tanh,
+            )
+            if e < E1 - 1:
+                cb = ring.tile([P, H], BF16, name="cb")
+            else:
+                cb = keep.tile([P, H], BF16, name="cb_last", tag="late", align_bytes=64)
+            nc.scalar.activation(cb[:], hs[:], ACT.Copy, scale=g1[:, e : e + 1])
+            words = cb[:].bitcast(F32)
+            tr = psum.tile([P, 2, C1], F32, name="tr", tag="tr", bufs=2)
+            for u in range(2):
+                nc.tensor.transpose(tr[:, u, :], words[:, u * P : (u + 1) * P], ident[:])
+            cw = ring.tile([P, 2, C1], F32, name="cw")
+            nc.scalar.copy(cw[:], tr[:])
+            for u in range(2):
+                nc.vector.tensor_copy(cwin[u][:].indirect(list1[:, e * C1 // 16 : (e + 1) * C1 // 16]), cw[:, u, :])
+
+        g2 = keep.tile([P, T], F32, name="g2", tag="d", align_bytes=64)
+        nc.sync.dma_start(g2[:], gate2)
+        w2g = keep.tile([P, E2 * N * PACK], BF16, name="w2g", tag="late", align_bytes=64)
+
+        def prepare_w2(f):
+            part = w2g[:, f * N * PACK : (f + 1) * N * PACK]
+            nc.scalar.copy(
+                part.rearrange("p (t m j) -> p m j t", t=PACK, j=PACK),
+                w2raw[f][:].rearrange("p j (m t) -> p m j t", t=PACK),
+            )
+            nc.vector.quantize_mx(out=w2q[f][:].bitcast(FP8X4), scales=w2s[f][:], in_=part)
+
+        prepare_w2(0)
+        cin_all = keep.tile([P, T * PACK], BF16, name="cin_all", tag="c", align_bytes=64)
+
+        y = keep.tile([P, PACK, T], F32, name="y")
+        for f in range(E2):
+            if f > 0:
+                prepare_w2(f)
+            cin = cin_all[:, f * C2 * PACK : (f + 1) * C2 * PACK]
+            pairs = cin.bitcast(U32).rearrange("p (m u) -> p m u", u=2)
+            for u in range(2):
+                nc.vector.tensor_copy(
+                    pairs[:, :, u], cwin[u][:].bitcast(U32).indirect(list2[:, f * COLS : (f + 1) * COLS])
+                )
+            cq = ring.tile([P, C2], U32, name="cq", align_bytes=64)
+            cs = ring.tile([P, C2], U8, name="cs", align_bytes=64)
+            nc.vector.quantize_mx(out=cq[:].bitcast(FP8X4), scales=cs[:], in_=cin)
+            for half in range(2):
+                bank = psum.tile([P, 2, C2], F32, name="bank", tag="bank", bufs=3)
+                for tt in range(2):
+                    t = 2 * half + tt
+                    nc.tensor.matmul_mx(
+                        out=bank[:, tt, :],
+                        lhsT=w2q[f][:, t * P : (t + 1) * P].bitcast(FP8X4),
+                        lhsT_scale=w2s[f][:, t * P : (t + 1) * P],
+                        rhs=cq[:].bitcast(FP8X4),
+                        rhs_scale=cs[:],
+                        start=True,
+                        stop=True,
+                    )
+                nc.scalar.copy(y[:, 2 * half : 2 * half + 2, f * C2 : (f + 1) * C2], bank[:])
+
+        owin = [keep.tile([P, WIDE], F32, name="owin%d" % t) for t in range(PACK)]
+        for f in range(E2):
+            cols = slice(f * C2, (f + 1) * C2)
+            for t in range(2):
+                nc.vector.tensor_tensor(
+                    owin[t][:].indirect(list2[:, f * COLS : (f + 1) * COLS]), y[:, t, cols], g2[:, cols], MULT
+                )
+        for t in range(2, PACK):
+            nc.vector.tensor_tensor(owin[t][:].indirect(list2[:]), y[:, t, :], g2[:], MULT)
+
+        out_rows = out_0.rearrange("(p t) m -> t p m", t=PACK)
+        ob = keep.tile([P, T, PACK], BF16, name="ob", align_bytes=64)
+        for t in range(PACK):
+            nc.sync.dma_start(out_rows[t], owin[t][:, 0:T])
+            if t < 2:
+                nc.scalar.copy(ob[:, :, t], owin[t][:, 0:T])
+            elif t == 2:
+                nc.scalar.copy(ob[:, :, 2:4], owin[t][:, 0:T].unsqueeze(2).to_broadcast([P, T, 2]))
+        ow = keep.tile([P, T], U32, name="ow", align_bytes=64)
+        osc = keep.tile([P, T], U8, name="osc", align_bytes=64)
+        word_rows = out_1[0].rearrange("p m d -> p (m d)").bitcast(I32)
+        nc.scalar.copy(ob[:, 0:CHUNK, 3], owin[3][:, 0:CHUNK])
+        for k in range(1, CHUNKS):
+            cols = slice(k * CHUNK, (k + 1) * CHUNK)
+            nc.vector.tensor_copy(ob[:, cols, 3], owin[3][:, cols])
+        for k in range(CHUNKS):
+            cols = slice(k * CHUNK, (k + 1) * CHUNK)
+            nc.vector.quantize_mx(
+                out=ow[:, cols].bitcast(FP8X4),
+                scales=osc[:, cols],
+                in_=ob[:, cols, :].rearrange("p m t -> p (m t)"),
+            )
+            nc.sync.dma_start(word_rows[:, cols], ow[:, cols].bitcast(I32))
+        scale_rows = out_2[0].rearrange("(q r) m -> r q m", r=4)
+        for r in range(4):
+            queue = nc.scalar if r % 2 else nc.sync
+            queue.dma_start(scale_rows[r].bitcast(I32), osc[r:P:32, :].bitcast(I32))

@@ -41,15 +41,14 @@ def tile_moe_ser_gelu_kernel(
         list1 = lists.tile([P, T // 16], U16, name="list1")
         list2 = lists.tile([P, T // 16], U16, name="list2")
 
-        xs = keep.tile([P, PASSES * T], U8, name="xs", align_bytes=64)
-        nc.gpsimd.memset(xs[:].bitcast(I32), 0)
-        w1s = keep.tile([P, E1 * PASSES * H], U8, name="w1s", align_bytes=64)
-        nc.vector.memset(w1s[:].bitcast(I32), 0)
-        g1rows = keep.tile([P, P], F32, name="g1rows", tag="a", align_bytes=64)
-        nc.gpsimd.memset(g1rows[:], 0.0)
-        nc.gpsimd.dma_start(g1rows[0:E1, :], gate1[0].rearrange("(e u) -> e u", e=E1))
         ident = keep.tile([P, P], F32, name="ident")
         make_identity(nc, ident[:])
+        xs = keep.tile([P, PASSES * T], U8, name="xs", align_bytes=64)
+        nc.vector.memset(xs[:].bitcast(I32), 0)
+        g1rows = keep.tile([P, P], F32, name="g1rows", tag="a", align_bytes=64)
+        nc.vector.memset(g1rows[:], 0.0)
+        w1s = keep.tile([P, E1 * PASSES * H], U8, name="w1s", align_bytes=64)
+        nc.vector.memset(w1s[:].bitcast(I32), 0)
         warm = keep.tile([P, 1], F32, name="warm")
         nc.scalar.activation(warm[:], ident[:, 0:1], ACT.Gelu_apprx_tanh)
 
@@ -65,6 +64,7 @@ def tile_moe_ser_gelu_kernel(
             nc.sync.dma_start(
                 xs[r:P:32, :].bitcast(I32).rearrange("q (s t) -> q s t", s=PASSES), xs_rows[r].bitcast(I32)
             )
+        nc.scalar.dma_start(g1rows[0:E1, :], gate1[0].rearrange("(e u) -> e u", e=E1))
         w1s_rows = w1_scales.rearrange("e s (q r) n -> r q (e s) n", r=4)
 
         def load_w1_scales(e0, e1):
@@ -174,46 +174,55 @@ def tile_moe_ser_gelu_kernel(
             )
             nc.vector.quantize_mx(out=w2q[f][:].bitcast(FP8X4), scales=w2s[f][:], in_=part)
 
-        prepare_w2(0)
-        cin_all = keep.tile([P, T * PACK], BF16, name="cin_all", tag="c", align_bytes=64)
+        cq, cs = [], []
 
-        y = keep.tile([P, PACK, T], F32, name="y")
-        for f in range(E2):
-            if f > 0:
-                prepare_w2(f)
-            cin = cin_all[:, f * C2 * PACK : (f + 1) * C2 * PACK]
-            pairs = cin.bitcast(U32).rearrange("p (m u) -> p m u", u=2)
+        def gather_c(f):
+            cin = keep.tile([P, C2 * PACK], BF16, name="cin%d" % f, tag="fgc"[f], align_bytes=64)
+            pairs = cin[:].bitcast(U32).rearrange("p (m u) -> p m u", u=2)
             for u in range(2):
                 nc.vector.tensor_copy(
                     pairs[:, :, u], cwin[u][:].bitcast(U32).indirect(list2[:, f * COLS : (f + 1) * COLS])
                 )
-            cq = ring.tile([P, C2], U32, name="cq", align_bytes=64)
-            cs = ring.tile([P, C2], U8, name="cs", align_bytes=64)
-            nc.vector.quantize_mx(out=cq[:].bitcast(FP8X4), scales=cs[:], in_=cin)
-            for half in range(2):
-                bank = psum.tile([P, 2, C2], F32, name="bank", tag="bank", bufs=3)
-                for tt in range(2):
-                    t = 2 * half + tt
-                    nc.tensor.matmul_mx(
-                        out=bank[:, tt, :],
-                        lhsT=w2q[f][:, t * P : (t + 1) * P].bitcast(FP8X4),
-                        lhsT_scale=w2s[f][:, t * P : (t + 1) * P],
-                        rhs=cq[:].bitcast(FP8X4),
-                        rhs_scale=cs[:],
-                        start=True,
-                        stop=True,
-                    )
-                nc.scalar.copy(y[:, 2 * half : 2 * half + 2, f * C2 : (f + 1) * C2], bank[:])
+            cq.append(keep.tile([P, C2], U32, name="cq%d" % f, align_bytes=64))
+            cs.append(keep.tile([P, C2], U8, name="cs%d" % f, align_bytes=64))
+            nc.vector.quantize_mx(out=cq[f][:].bitcast(FP8X4), scales=cs[f][:], in_=cin[:])
+
+        def product(f, half):
+            bank = psum.tile([P, 2, C2], F32, name="bank", tag="bank", bufs=3)
+            for tt in range(2):
+                t = 2 * half + tt
+                nc.tensor.matmul_mx(
+                    out=bank[:, tt, :],
+                    lhsT=w2q[f][:, t * P : (t + 1) * P].bitcast(FP8X4),
+                    lhsT_scale=w2s[f][:, t * P : (t + 1) * P],
+                    rhs=cq[f][:].bitcast(FP8X4),
+                    rhs_scale=cs[f][:],
+                    start=True,
+                    stop=True,
+                )
+            return bank
 
         owin = [keep.tile([P, WIDE], F32, name="owin%d" % t) for t in range(PACK)]
+        y_late = keep.tile([P, 2, T], F32, name="y_late")
+
+        gather_c(0)
+        gather_c(1)
+        prepare_w2(0)
+        gather_c(2)
+        prepare_w2(1)
         for f in range(E2):
             cols = slice(f * C2, (f + 1) * C2)
+            y = keep.tile([P, 2, C2], F32, name="y%d" % f, tag="hbi"[f], align_bytes=64)
+            nc.scalar.copy(y[:], product(f, 0)[:])
             for t in range(2):
                 nc.vector.tensor_tensor(
-                    owin[t][:].indirect(list2[:, f * COLS : (f + 1) * COLS]), y[:, t, cols], g2[:, cols], MULT
+                    owin[t][:].indirect(list2[:, f * COLS : (f + 1) * COLS]), y[:, t, :], g2[:, cols], MULT
                 )
+            if f == 0:
+                prepare_w2(2)
+            nc.scalar.copy(y_late[:, :, cols], product(f, 1)[:])
         for t in range(2, PACK):
-            nc.vector.tensor_tensor(owin[t][:].indirect(list2[:]), y[:, t, :], g2[:], MULT)
+            nc.vector.tensor_tensor(owin[t][:].indirect(list2[:]), y_late[:, t - 2, :], g2[:], MULT)
 
         out_rows = out_0.rearrange("(p t) m -> t p m", t=PACK)
         ob = keep.tile([P, T, PACK], BF16, name="ob", align_bytes=64)

@@ -43,105 +43,119 @@ def tile_moe_ser_gelu_kernel(
 
         ident = keep.tile([P, P], F32, name="ident")
         make_identity(nc, ident[:])
-        xs = keep.tile([P, PASSES * T], U8, name="xs", align_bytes=64)
+        xs = keep.tile([P, PASSES * T], U8, name="xs", tag="xs", align_bytes=64)
         nc.vector.memset(xs[:].bitcast(I32), 0)
+        w1s_first = keep.tile([P, 2 * PASSES * H], U8, name="w1s_first", tag="d", align_bytes=64)
+        nc.vector.memset(w1s_first[:].bitcast(I32), 0)
         g1rows = keep.tile([P, P], F32, name="g1rows", tag="a", align_bytes=64)
         nc.vector.memset(g1rows[:], 0.0)
-        w1s = keep.tile([P, E1 * PASSES * H], U8, name="w1s", align_bytes=64)
-        nc.vector.memset(w1s[:].bitcast(I32), 0)
+        w1s_rest = keep.tile([P, (E1 - 2) * PASSES * H], U8, name="w1s_rest", align_bytes=64)
+        nc.vector.memset(w1s_rest[:].bitcast(I32), 0)
         warm = keep.tile([P, 1], F32, name="warm")
         nc.scalar.activation(warm[:], ident[:, 0:1], ACT.Gelu_apprx_tanh)
 
-        nc.sync.dma_start(list1[:], offs)
-        nc.sync.dma_start(list2[:], offs2)
         x_rows = x_words.rearrange("s p t d -> p s (t d)").bitcast(I32)
         xw0 = keep.tile([P, T], I32, name="xw0", tag="b", align_bytes=64)
         nc.sync.dma_start(xw0[:], x_rows[:, 0, :])
-        xw = keep.tile([P, (PASSES - 1) * T], I32, name="xw", tag="c", align_bytes=64)
+        nc.sync.dma_start(list1[:], offs)
+        nc.sync.dma_start(list2[:], offs2)
+        xw = keep.tile([P, (PASSES - 1) * T], I32, name="xw", align_bytes=64)
         nc.sync.dma_start(xw[:].rearrange("p (s t) -> p s t", s=PASSES - 1), x_rows[:, 1:PASSES, :])
         xs_rows = x_scales.rearrange("s (q r) t -> r q s t", r=4)
         for r in range(4):
             nc.sync.dma_start(
                 xs[r:P:32, :].bitcast(I32).rearrange("q (s t) -> q s t", s=PASSES), xs_rows[r].bitcast(I32)
             )
-        nc.scalar.dma_start(g1rows[0:E1, :], gate1[0].rearrange("(e u) -> e u", e=E1))
         w1s_rows = w1_scales.rearrange("e s (q r) n -> r q (e s) n", r=4)
 
-        def load_w1_scales(e0, e1):
+        def load_w1_scales(planes, e0, e1):
             g0, g1 = e0 * PASSES, e1 * PASSES
             for r in range(4):
                 nc.sync.dma_start(
-                    w1s[r:P:32, g0 * H : g1 * H].bitcast(I32).rearrange("q (g n) -> q g n", g=g1 - g0),
+                    planes[r:P:32, :].bitcast(I32).rearrange("q (g n) -> q g n", g=g1 - g0),
                     w1s_rows[r][:, g0:g1, :].bitcast(I32),
                 )
 
 
-        w1w = []
-        w2raw = []
+        PAIR = 2 * PASSES * 2 * H
 
-        def load_w1(k):
-            w1w.append(keep.tile([P, 2 * PASSES * 2 * H], U8, name="w1w%d" % k, tag="eba"[k], align_bytes=64))
+        def load_w1(tile, k):
             nc.sync.dma_start(
-                w1w[k][:].bitcast(I32).rearrange("p (g n) -> p g n", g=2 * PASSES),
+                tile.bitcast(I32).rearrange("p (g n) -> p g n", g=2 * PASSES),
                 w1_words[2 * k : 2 * k + 2].rearrange("e s p n -> p (e s) n").bitcast(I32),
             )
 
-        def load_w2(f):
-            w2raw.append(keep.tile([P, PACK, N], F32, name="w2raw%d" % f, tag="ceb"[f], align_bytes=64))
-            nc.sync.dma_start(w2raw[f][:], w2[f].rearrange("(p j) n -> p j n", j=PACK))
-
-        load_w1(0)
-        load_w1_scales(0, E1)
+        w1_first = keep.tile([P, PAIR], U8, name="w1_first", align_bytes=64)
+        load_w1(w1_first[:], 0)
+        load_w1_scales(w1s_first, 0, 2)
+        nc.sync.dma_start(g1rows[0:E1, :], gate1[0].rearrange("(e u) -> e u", e=E1))
 
         gt = psum.tile([P, P], F32, name="gt", tag="tr", bufs=2)
         nc.tensor.transpose(gt[:], g1rows[:], ident[:])
         g1 = keep.tile([P, 8], F32, name="g1")
         nc.scalar.copy(g1[:, 0:E1], gt[:, 0:E1])
 
-        xg0 = keep.tile([P, T], U32, name="xg0", tag="d", align_bytes=64)
+        xg0 = keep.tile([P, T], U32, name="xg0", align_bytes=64)
         for a in range(0, T, T // 2):
             nc.vector.tensor_copy(
                 xg0[:, a : a + T // 2], xw0[:].bitcast(U32).indirect(list1[:, a // 16 : (a + T // 2) // 16])
             )
-        load_w1(1)
-        load_w1(2)
-        xg12 = keep.tile([P, (PASSES - 1) * T], U32, name="xg12", align_bytes=64)
+        w1_rest = keep.tile([P, 2 * PAIR], U8, name="w1_rest", tag="b", align_bytes=64)
+        w1w = [w1_first[:], w1_rest[:, 0:PAIR], w1_rest[:, PAIR : 2 * PAIR]]
+        load_w1(w1w[1], 1)
+        load_w1_scales(w1s_rest, 2, E1)
+        load_w1(w1w[2], 2)
+        w2_all = keep.tile([P, E2 * PACK * N], F32, name="w2_all", tag="a", align_bytes=64)
+        w2raw = [w2_all[:, f * PACK * N : (f + 1) * PACK * N].rearrange("p (j n) -> p j n", j=PACK) for f in range(E2)]
+        for f in range(E2):
+            nc.sync.dma_start(w2raw[f], w2[f].rearrange("(p j) n -> p j n", j=PACK))
+        REST = T - CHUNK
+        xga = keep.tile([P, (PASSES - 1) * CHUNK], U32, name="xga", align_bytes=64)
         for s in range(PASSES - 1):
-            for a in range(0, T, T // 2):
-                nc.vector.tensor_copy(
-                    xg12[:, s * T + a : s * T + a + T // 2],
-                    xw[:, s * T : (s + 1) * T].bitcast(U32).indirect(list1[:, a // 16 : (a + T // 2) // 16]),
-                )
-        load_w2(0)
-        xg = [xg0[:], xg12[:, 0:T], xg12[:, T : 2 * T]]
+            nc.vector.tensor_copy(
+                xga[:, s * CHUNK : (s + 1) * CHUNK],
+                xw[:, s * T : (s + 1) * T].bitcast(U32).indirect(list1[:, 0:COLS]),
+            )
         sg = [keep.tile([P, T], U8, name="sg%d" % s, align_bytes=64) for s in range(PASSES)]
-        for a in range(0, T, CHUNK):
+        for a, b in ((0, CHUNK), (CHUNK, T)):
             for s in range(PASSES):
+                nc.vector.tensor_copy(sg[s][:, a:b], xs[:, s * T : (s + 1) * T].indirect(list1[:, a // 16 : b // 16]))
+        xgb = keep.tile([P, (PASSES - 1) * REST], U32, name="xgb", tag="xs", align_bytes=64)
+        for a in range(0, REST, CHUNK):
+            for s in range(PASSES - 1):
                 nc.vector.tensor_copy(
-                    sg[s][:, a : a + CHUNK], xs[:, s * T : (s + 1) * T].indirect(list1[:, a // 16 : (a + CHUNK) // 16])
+                    xgb[:, s * REST + a : s * REST + a + CHUNK],
+                    xw[:, s * T : (s + 1) * T].bitcast(U32).indirect(list1[:, (CHUNK + a) // 16 : (2 * CHUNK + a) // 16]),
                 )
 
-        w2q = [keep.tile([P, N], U32, name="w2q%d" % f, align_bytes=64) for f in range(E2)]
-        w2s = [keep.tile([P, N], U8, name="w2s%d" % f, align_bytes=64) for f in range(E2)]
+        def slot_words(s, e):
+            if s == 0:
+                return xg0[:, e * C1 : (e + 1) * C1]
+            if e * C1 < CHUNK:
+                return xga[:, (s - 1) * CHUNK + e * C1 : (s - 1) * CHUNK + (e + 1) * C1]
+            a = (s - 1) * REST + e * C1 - CHUNK
+            return xgb[:, a : a + C1]
 
         cwin = [keep.tile([P, T], F32, name="cwin%d" % u) for u in range(2)]
         for e in range(E1):
             k, ee = divmod(e, 2)
             slots = slice(e * C1, (e + 1) * C1)
+            planes, first = (w1s_first, e * PASSES) if e < 2 else (w1s_rest, (e - 2) * PASSES)
             acc = psum.tile([P, H], F32, name="acc", tag="acc", bufs=3)
             for s in range(PASSES):
                 g = ee * PASSES + s
                 nc.tensor.matmul_mx(
                     out=acc[:],
-                    lhsT=xg[s][:, slots].bitcast(FP8X4),
+                    lhsT=slot_words(s, e).bitcast(FP8X4),
                     lhsT_scale=sg[s][:, slots],
                     rhs=w1w[k][:, g * 2 * H : (g + 1) * 2 * H].bitcast(FP4X4),
-                    rhs_scale=w1s[:, (e * PASSES + s) * H : (e * PASSES + s + 1) * H],
+                    rhs_scale=planes[:, (first + s) * H : (first + s + 1) * H],
                     start=(s == 0),
                     stop=(s == PASSES - 1),
                 )
-            if e in (1, 3):
-                load_w2((e + 1) // 2)
+            if e == 1:
+                g2 = keep.tile([P, T], F32, name="g2", tag="d", align_bytes=64)
+                nc.sync.dma_start(g2[:], gate2)
             hs = ring.tile([P, H], F32, name="hs")
             nc.scalar.activation(
                 hs[:].rearrange("s (u p d) -> s u p d", u=2, d=2),
@@ -162,39 +176,44 @@ def tile_moe_ser_gelu_kernel(
             for u in range(2):
                 nc.vector.tensor_copy(cwin[u][:].indirect(list1[:, e * C1 // 16 : (e + 1) * C1 // 16]), cw[:, u, :])
 
-        g2 = keep.tile([P, T], F32, name="g2", tag="d", align_bytes=64)
-        nc.sync.dma_start(g2[:], gate2)
-        w2g = keep.tile([P, E2 * N * PACK], BF16, name="w2g", tag="late", align_bytes=64)
+        HALF = N // 2
+        w2q, w2s = {}, {}
 
-        def prepare_w2(f):
-            part = w2g[:, f * N * PACK : (f + 1) * N * PACK]
+        def prepare_w2(rounded, f, half):
+            part = rounded[:, f * HALF * PACK : (f + 1) * HALF * PACK]
             nc.scalar.copy(
-                part.rearrange("p (t m j) -> p m j t", t=PACK, j=PACK),
-                w2raw[f][:].rearrange("p j (m t) -> p m j t", t=PACK),
+                part.rearrange("p (t m j) -> p m j t", t=2, j=PACK),
+                w2raw[f].rearrange("p j (m t) -> p m j t", t=PACK)[:, :, :, 2 * half : 2 * half + 2],
             )
-            nc.vector.quantize_mx(out=w2q[f][:].bitcast(FP8X4), scales=w2s[f][:], in_=part)
+            name = "w2%s%d%d"
+            w2q[f, half] = keep.tile([P, HALF], U32, name=name % ("q", f, half), tag=name % ("q", f, half), align_bytes=64)
+            w2s[f, half] = keep.tile([P, HALF], U8, name=name % ("s", f, half), tag=name % ("s", f, half), align_bytes=64)
+            nc.vector.quantize_mx(out=w2q[f, half][:].bitcast(FP8X4), scales=w2s[f, half][:], in_=part)
 
         cq, cs = [], []
 
         def gather_c(f):
-            cin = keep.tile([P, C2 * PACK], BF16, name="cin%d" % f, tag="fgc"[f], align_bytes=64)
-            pairs = cin[:].bitcast(U32).rearrange("p (m u) -> p m u", u=2)
+            pairs = ring.tile([P, 2, C2], U32, name="pairs", bufs=2)
             for u in range(2):
                 nc.vector.tensor_copy(
-                    pairs[:, :, u], cwin[u][:].bitcast(U32).indirect(list2[:, f * COLS : (f + 1) * COLS])
+                    pairs[:, u, :], cwin[u][:].bitcast(U32).indirect(list2[:, f * COLS : (f + 1) * COLS])
                 )
-            cq.append(keep.tile([P, C2], U32, name="cq%d" % f, align_bytes=64))
+            return pairs
+
+        def quantize_c(f, pairs):
+            cin = keep.tile([P, C2 * PACK], BF16, name="cin%d" % f, tag=("cin0", "cin1", "w2q10")[f], align_bytes=64)
+            nc.scalar.copy(cin[:].bitcast(U32).rearrange("p (m u) -> p m u", u=2), pairs[:].rearrange("p u m -> p m u"))
+            cq.append(keep.tile([P, C2], U32, name="cq%d" % f, tag="jkh"[f], align_bytes=64))
             cs.append(keep.tile([P, C2], U8, name="cs%d" % f, align_bytes=64))
             nc.vector.quantize_mx(out=cq[f][:].bitcast(FP8X4), scales=cs[f][:], in_=cin[:])
 
         def product(f, half):
             bank = psum.tile([P, 2, C2], F32, name="bank", tag="bank", bufs=3)
             for tt in range(2):
-                t = 2 * half + tt
                 nc.tensor.matmul_mx(
                     out=bank[:, tt, :],
-                    lhsT=w2q[f][:, t * P : (t + 1) * P].bitcast(FP8X4),
-                    lhsT_scale=w2s[f][:, t * P : (t + 1) * P],
+                    lhsT=w2q[f, half][:, tt * P : (tt + 1) * P].bitcast(FP8X4),
+                    lhsT_scale=w2s[f, half][:, tt * P : (tt + 1) * P],
                     rhs=cq[f][:].bitcast(FP8X4),
                     rhs_scale=cs[f][:],
                     start=True,
@@ -205,22 +224,31 @@ def tile_moe_ser_gelu_kernel(
         owin = [keep.tile([P, WIDE], F32, name="owin%d" % t) for t in range(PACK)]
         y_late = keep.tile([P, 2, T], F32, name="y_late")
 
-        gather_c(0)
-        gather_c(1)
-        prepare_w2(0)
-        gather_c(2)
-        prepare_w2(1)
+        rounded = keep.tile([P, E2 * HALF * PACK], BF16, name="rounded0", tag="late", align_bytes=64)
         for f in range(E2):
+            prepare_w2(rounded, f, 0)
+        quantize_c(0, gather_c(0))
+        quantize_c(1, gather_c(1))
+        last_pairs = gather_c(2)
+
+        def early_rows(f):
             cols = slice(f * C2, (f + 1) * C2)
-            y = keep.tile([P, 2, C2], F32, name="y%d" % f, tag="hbi"[f], align_bytes=64)
+            y = keep.tile([P, 2, C2], F32, name="y%d" % f, tag=("h", "y1", "y2")[f], align_bytes=64)
             nc.scalar.copy(y[:], product(f, 0)[:])
             for t in range(2):
                 nc.vector.tensor_tensor(
                     owin[t][:].indirect(list2[:, f * COLS : (f + 1) * COLS]), y[:, t, :], g2[:, cols], MULT
                 )
-            if f == 0:
-                prepare_w2(2)
-            nc.scalar.copy(y_late[:, :, cols], product(f, 1)[:])
+
+        early_rows(0)
+        quantize_c(2, last_pairs)
+        rounded = keep.tile([P, E2 * HALF * PACK], BF16, name="rounded1", tag="w2s10", align_bytes=64)
+        prepare_w2(rounded, 0, 1)
+        for f in range(1, E2):
+            prepare_w2(rounded, f, 1)
+            early_rows(f)
+        for f in range(E2):
+            nc.scalar.copy(y_late[:, :, f * C2 : (f + 1) * C2], product(f, 1)[:])
         for t in range(2, PACK):
             nc.vector.tensor_tensor(owin[t][:].indirect(list2[:]), y_late[:, t - 2, :], g2[:], MULT)
 

from contextlib import ExitStack

import concourse.mybir as mybir
from concourse.masks import make_identity

K, T, H, N = 1536, 768, 512, 512
E1, C1 = 6, 128
E2, C2 = 3, 256
FLOPS = 2 * T * K * H + 2 * T * H * N

F32 = mybir.dt.float32
BF16 = mybir.dt.bfloat16
I32 = mybir.dt.int32
U32 = mybir.dt.uint32
U16 = mybir.dt.uint16
U8 = mybir.dt.uint8
FP8X4 = mybir.dt.float8_e4m3fn_x4
FP4X4 = mybir.dt.float4_e2m1fn_x4
ACT = mybir.ActivationFunctionType
MULT = mybir.AluOpType.mult

P = 128
PACK = 4
PASSES = K // (P * PACK)
CHUNK = 256
CHUNKS = T // CHUNK
COLS = CHUNK // 16
WIDE = 1024


def tile_moe_ser_gelu_kernel(
    tc, x_words, x_scales, w1_words, w1_scales, w2, gate1, gate2, offs, offs2, out_0, out_1, out_2
):
    nc = tc.nc
    with ExitStack() as ctx:
        lists = ctx.enter_context(tc.tile_pool(name="lists", bufs=1))
        keep = ctx.enter_context(tc.tile_pool(name="keep", bufs=1))
        ring = ctx.enter_context(tc.tile_pool(name="ring", bufs=3))
        psum = ctx.enter_context(tc.psum_pool(name="psum", bufs=1))

        list1 = lists.tile([P, T // 16], U16, name="list1")
        list2 = lists.tile([P, T // 16], U16, name="list2")

        ident = keep.tile([P, P], F32, name="ident")
        make_identity(nc, ident[:])
        xs = keep.tile([P, PASSES * T], U8, name="xs", tag="xs", align_bytes=64)
        nc.vector.memset(xs[:].bitcast(I32), 0)
        w1s_first = keep.tile([P, 2 * PASSES * H], U8, name="w1s_first", tag="d", align_bytes=64)
        nc.vector.memset(w1s_first[:].bitcast(I32), 0)
        g1rows = keep.tile([P, P], F32, name="g1rows", tag="a", align_bytes=64)
        nc.vector.memset(g1rows[:], 0.0)
        w1s_rest = keep.tile([P, (E1 - 2) * PASSES * H], U8, name="w1s_rest", align_bytes=64)
        nc.vector.memset(w1s_rest[:].bitcast(I32), 0)
        warm = keep.tile([P, 1], F32, name="warm")
        nc.scalar.activation(warm[:], ident[:, 0:1], ACT.Gelu_apprx_tanh)

        x_rows = x_words.rearrange("s p t d -> p s (t d)").bitcast(I32)
        xw0 = keep.tile([P, T], I32, name="xw0", tag="b", align_bytes=64)
        nc.sync.dma_start(xw0[:], x_rows[:, 0, :])
        nc.sync.dma_start(list1[:], offs)
        nc.sync.dma_start(list2[:], offs2)
        xw = keep.tile([P, (PASSES - 1) * T], I32, name="xw", align_bytes=64)
        nc.sync.dma_start(xw[:].rearrange("p (s t) -> p s t", s=PASSES - 1), x_rows[:, 1:PASSES, :])
        xs_rows = x_scales.rearrange("s (q r) t -> r q s t", r=4)
        for r in range(4):
            nc.sync.dma_start(
                xs[r:P:32, :].bitcast(I32).rearrange("q (s t) -> q s t", s=PASSES), xs_rows[r].bitcast(I32)
            )
        w1s_rows = w1_scales.rearrange("e s (q r) n -> r q (e s) n", r=4)

        def load_w1_scales(planes, e0, e1):
            g0, g1 = e0 * PASSES, e1 * PASSES
            for r in range(4):
                nc.sync.dma_start(
                    planes[r:P:32, :].bitcast(I32).rearrange("q (g n) -> q g n", g=g1 - g0),
                    w1s_rows[r][:, g0:g1, :].bitcast(I32),
                )


        PAIR = 2 * PASSES * 2 * H

        def load_w1(tile, k):
            nc.sync.dma_start(
                tile.bitcast(I32).rearrange("p (g n) -> p g n", g=2 * PASSES),
                w1_words[2 * k : 2 * k + 2].rearrange("e s p n -> p (e s) n").bitcast(I32),
            )

        w1_first = keep.tile([P, PAIR], U8, name="w1_first", align_bytes=64)
        load_w1(w1_first[:], 0)
        load_w1_scales(w1s_first, 0, 2)
        nc.sync.dma_start(g1rows[0:E1, :], gate1[0].rearrange("(e u) -> e u", e=E1))

        gt = psum.tile([P, P], F32, name="gt", tag="tr", bufs=2)
        nc.tensor.transpose(gt[:], g1rows[:], ident[:])
        g1 = keep.tile([P, 8], F32, name="g1")
        nc.scalar.copy(g1[:, 0:E1], gt[:, 0:E1])

        xg0 = keep.tile([P, T], U32, name="xg0", align_bytes=64)
        for a in range(0, T, T // 2):
            nc.vector.tensor_copy(
                xg0[:, a : a + T // 2], xw0[:].bitcast(U32).indirect(list1[:, a // 16 : (a + T // 2) // 16])
            )
        w1_rest = keep.tile([P, 2 * PAIR], U8, name="w1_rest", tag="b", align_bytes=64)
        w1w = [w1_first[:], w1_rest[:, 0:PAIR], w1_rest[:, PAIR : 2 * PAIR]]
        load_w1(w1w[1], 1)
        load_w1_scales(w1s_rest, 2, E1)
        load_w1(w1w[2], 2)
        w2_all = keep.tile([P, E2 * PACK * N], F32, name="w2_all", tag="a", align_bytes=64)
        w2raw = [w2_all[:, f * PACK * N : (f + 1) * PACK * N].rearrange("p (j n) -> p j n", j=PACK) for f in range(E2)]
        for f in range(E2):
            nc.sync.dma_start(w2raw[f], w2[f].rearrange("(p j) n -> p j n", j=PACK))
        REST = T - CHUNK
        xga = keep.tile([P, (PASSES - 1) * CHUNK], U32, name="xga", align_bytes=64)
        for s in range(PASSES - 1):
            nc.vector.tensor_copy(
                xga[:, s * CHUNK : (s + 1) * CHUNK],
                xw[:, s * T : (s + 1) * T].bitcast(U32).indirect(list1[:, 0:COLS]),
            )
        sg = [keep.tile([P, T], U8, name="sg%d" % s, align_bytes=64) for s in range(PASSES)]
        for a, b in ((0, CHUNK), (CHUNK, T)):
            for s in range(PASSES):
                nc.vector.tensor_copy(sg[s][:, a:b], xs[:, s * T : (s + 1) * T].indirect(list1[:, a // 16 : b // 16]))
        xgb = keep.tile([P, (PASSES - 1) * REST], U32, name="xgb", tag="xs", align_bytes=64)
        for a in range(0, REST, CHUNK):
            for s in range(PASSES - 1):
                nc.vector.tensor_copy(
                    xgb[:, s * REST + a : s * REST + a + CHUNK],
                    xw[:, s * T : (s + 1) * T].bitcast(U32).indirect(list1[:, (CHUNK + a) // 16 : (2 * CHUNK + a) // 16]),
                )

        def slot_words(s, e):
            if s == 0:
                return xg0[:, e * C1 : (e + 1) * C1]
            if e * C1 < CHUNK:
                return xga[:, (s - 1) * CHUNK + e * C1 : (s - 1) * CHUNK + (e + 1) * C1]
            a = (s - 1) * REST + e * C1 - CHUNK
            return xgb[:, a : a + C1]

        cwin = [keep.tile([P, T], F32, name="cwin%d" % u) for u in range(2)]
        for e in range(E1):
            k, ee = divmod(e, 2)
            slots = slice(e * C1, (e + 1) * C1)
            planes, first = (w1s_first, e * PASSES) if e < 2 else (w1s_rest, (e - 2) * PASSES)
            acc = psum.tile([P, H], F32, name="acc", tag="acc", bufs=3)
            for s in range(PASSES):
                g = ee * PASSES + s
                nc.tensor.matmul_mx(
                    out=acc[:],
                    lhsT=slot_words(s, e).bitcast(FP8X4),
                    lhsT_scale=sg[s][:, slots],
                    rhs=w1w[k][:, g * 2 * H : (g + 1) * 2 * H].bitcast(FP4X4),
                    rhs_scale=planes[:, (first + s) * H : (first + s + 1) * H],
                    start=(s == 0),
                    stop=(s == PASSES - 1),
                )
            if e == 1:
                g2 = keep.tile([P, T], F32, name="g2", tag="d", align_bytes=64)
                nc.sync.dma_start(g2[:], gate2)
            hs = ring.tile([P, H], F32, name="hs")
            nc.scalar.activation(
                hs[:].rearrange("s (u p d) -> s u p d", u=2, d=2),
                acc[:].rearrange("s (p u d) -> s u p d", u=2, d=2),
                ACT.Gelu_apprx_tanh,
            )
            if e < E1 - 1:
                cb = ring.tile([P, H], BF16, name="cb")
            else:
                cb = keep.tile([P, H], BF16, name="cb_last", tag="late", align_bytes=64)
            nc.scalar.activation(cb[:], hs[:], ACT.Copy, scale=g1[:, e : e + 1])
            words = cb[:].bitcast(F32)
            tr = psum.tile([P, 2, C1], F32, name="tr", tag="tr", bufs=2)
            for u in range(2):
                nc.tensor.transpose(tr[:, u, :], words[:, u * P : (u + 1) * P], ident[:])
            cw = ring.tile([P, 2, C1], F32, name="cw")
            nc.scalar.copy(cw[:], tr[:])
            for u in range(2):
                nc.vector.tensor_copy(cwin[u][:].indirect(list1[:, e * C1 // 16 : (e + 1) * C1 // 16]), cw[:, u, :])

        HALF = N // 2
        w2q, w2s = {}, {}

        def prepare_w2(rounded, f, half):
            part = rounded[:, f * HALF * PACK : (f + 1) * HALF * PACK]
            nc.scalar.copy(
                part.rearrange("p (t m j) -> p m j t", t=2, j=PACK),
                w2raw[f].rearrange("p j (m t) -> p m j t", t=PACK)[:, :, :, 2 * half : 2 * half + 2],
            )
            name = "w2%s%d%d"
            w2q[f, half] = keep.tile([P, HALF], U32, name=name % ("q", f, half), tag=name % ("q", f, half), align_bytes=64)
            w2s[f, half] = keep.tile([P, HALF], U8, name=name % ("s", f, half), tag=name % ("s", f, half), align_bytes=64)
            nc.vector.quantize_mx(out=w2q[f, half][:].bitcast(FP8X4), scales=w2s[f, half][:], in_=part)

        cq, cs = [], []

        def gather_c(f):
            pairs = ring.tile([P, 2, C2], U32, name="pairs", bufs=2)
            for u in range(2):
                nc.vector.tensor_copy(
                    pairs[:, u, :], cwin[u][:].bitcast(U32).indirect(list2[:, f * COLS : (f + 1) * COLS])
                )
            return pairs

        def quantize_c(f, pairs):
            cin = keep.tile([P, C2 * PACK], BF16, name="cin%d" % f, tag=("cin0", "cin1", "w2q10")[f], align_bytes=64)
            nc.scalar.copy(cin[:].bitcast(U32).rearrange("p (m u) -> p m u", u=2), pairs[:].rearrange("p u m -> p m u"))
            cq.append(keep.tile([P, C2], U32, name="cq%d" % f, tag="jkh"[f], align_bytes=64))
            cs.append(keep.tile([P, C2], U8, name="cs%d" % f, align_bytes=64))
            nc.vector.quantize_mx(out=cq[f][:].bitcast(FP8X4), scales=cs[f][:], in_=cin[:])

        def product(f, half):
            bank = psum.tile([P, 2, C2], F32, name="bank", tag="bank", bufs=3)
            for tt in range(2):
                nc.tensor.matmul_mx(
                    out=bank[:, tt, :],
                    lhsT=w2q[f, half][:, tt * P : (tt + 1) * P].bitcast(FP8X4),
                    lhsT_scale=w2s[f, half][:, tt * P : (tt + 1) * P],
                    rhs=cq[f][:].bitcast(FP8X4),
                    rhs_scale=cs[f][:],
                    start=True,
                    stop=True,
                )
            return bank

        owin = [keep.tile([P, WIDE], F32, name="owin%d" % t) for t in range(PACK)]
        y_late = keep.tile([P, 2, T], F32, name="y_late")

        rounded = keep.tile([P, E2 * HALF * PACK], BF16, name="rounded0", tag="late", align_bytes=64)
        for f in range(E2):
            prepare_w2(rounded, f, 0)
        quantize_c(0, gather_c(0))
        quantize_c(1, gather_c(1))
        last_pairs = gather_c(2)

        def early_rows(f):
            cols = slice(f * C2, (f + 1) * C2)
            y = keep.tile([P, 2, C2], F32, name="y%d" % f, tag=("h", "y1", "y2")[f], align_bytes=64)
            nc.scalar.copy(y[:], product(f, 0)[:])
            for t in range(2):
                nc.vector.tensor_tensor(
                    owin[t][:].indirect(list2[:, f * COLS : (f + 1) * COLS]), y[:, t, :], g2[:, cols], MULT
                )

        early_rows(0)
        quantize_c(2, last_pairs)
        rounded = keep.tile([P, E2 * HALF * PACK], BF16, name="rounded1", tag="w2s10", align_bytes=64)
        prepare_w2(rounded, 0, 1)
        for f in range(1, E2):
            prepare_w2(rounded, f, 1)
            early_rows(f)
        for f in range(E2):
            nc.scalar.copy(y_late[:, :, f * C2 : (f + 1) * C2], product(f, 1)[:])
        for t in range(2, PACK):
            nc.vector.tensor_tensor(owin[t][:].indirect(list2[:]), y_late[:, t - 2, :], g2[:], MULT)

        out_rows = out_0.rearrange("(p t) m -> t p m", t=PACK)
        ob = keep.tile([P, T, PACK], BF16, name="ob", align_bytes=64)
        for t in range(PACK):
            nc.sync.dma_start(out_rows[t], owin[t][:, 0:T])
            if t < 2:
                nc.scalar.copy(ob[:, :, t], owin[t][:, 0:T])
            elif t == 2:
                nc.scalar.copy(ob[:, :, 2:4], owin[t][:, 0:T].unsqueeze(2).to_broadcast([P, T, 2]))
        ow = keep.tile([P, T], U32, name="ow", align_bytes=64)
        osc = keep.tile([P, T], U8, name="osc", align_bytes=64)
        word_rows = out_1[0].rearrange("p m d -> p (m d)").bitcast(I32)
        nc.scalar.copy(ob[:, 0:CHUNK, 3], owin[3][:, 0:CHUNK])
        for k in range(1, CHUNKS):
            cols = slice(k * CHUNK, (k + 1) * CHUNK)
            nc.vector.tensor_copy(ob[:, cols, 3], owin[3][:, cols])
        for k in range(CHUNKS):
            cols = slice(k * CHUNK, (k + 1) * CHUNK)
            nc.vector.quantize_mx(
                out=ow[:, cols].bitcast(FP8X4),
                scales=osc[:, cols],
                in_=ob[:, cols, :].rearrange("p m t -> p (m t)"),
            )
            nc.sync.dma_start(word_rows[:, cols], ow[:, cols].bitcast(I32))
        scale_rows = out_2[0].rearrange("(q r) m -> r q m", r=4)
        for r in range(4):
            queue = nc.scalar if r % 2 else nc.sync
            queue.dma_start(scale_rows[r].bitcast(I32), osc[r:P:32, :].bitcast(I32))
